import numpy as np
import ml_dtypes


def mxq(x, axis, fmt="e4m3"):
    dtype, down = {"e4m3": (ml_dtypes.float8_e4m3fn, 7), "e5m2": (ml_dtypes.float8_e5m2, 14)}[fmt]
    v = np.moveaxis(np.asarray(x, np.float32).astype(ml_dtypes.bfloat16).astype(np.float64), axis, -1)
    blocks = v.reshape(v.shape[:-1] + (-1, 32))
    amax = np.abs(blocks).max(-1, keepdims=True)
    byte = np.maximum(np.where(amax > 0, np.frexp(amax)[1] - 1 + 127, 0) - down, 1)
    scale = np.exp2(byte - 127.0)
    codes = (blocks / scale).astype(np.float32).astype(dtype).astype(np.float64)
    return np.moveaxis((codes * scale).reshape(v.shape), -1, axis)


WIDE = False


def mx_kscale(k, group=512):
    if not WIDE:
        return np.ones(k)
    levels = np.array([10, -10, 5, -5, 0])
    if group != 512:
        return np.exp2(np.random.permutation(np.resize(levels, k // group))).repeat(group)
    if k % 512:
        return np.exp2(np.random.permutation(np.resize(levels, k // 32))).repeat(32)
    a = np.empty((k // 512, 16))
    for p in range(k // 512):
        a[p, :8] = np.random.permutation(np.resize(levels, 8))
        for g in range(8):
            far = levels[np.abs(levels - a[p, g]) >= 10]
            a[p, g + 8] = far[np.random.randint(len(far))]
    return np.exp2(a.ravel()).repeat(32)


def f64(x):
    return np.asarray(x).astype(np.float64)


def striped(idx):
    return np.tile(np.asarray(idx).reshape(-1, 16).T, (8, 1)).astype(np.uint16)


def unstriped(offs):
    return offs[:16].T.reshape(-1).astype(np.int64)


H, KV, D, NQ, N = 4, 2, 256, 512, 512


def setup_inputs():
    n = np.random.standard_normal
    s = mx_kscale(D, 0)[:, None]
    u = mx_kscale(N)
    t = np.random.uniform(0.5, 2.0, N) * u
    v = n((KV, N, 128))
    return {
        "qT": (n((H, D, NQ)) * s * (0.70 / np.sqrt(D))).astype(np.float32),
        "kT": (n((KV, D, N)) / s).astype(np.float32),
        "t": t.reshape(N, 1).astype(np.float32),
        "v": (v / t[:, None]).astype(np.float32),
        "gn": np.tile(np.random.uniform(0.5, 2.0, 128), (128, 1)).astype(np.float32),
        "og": n((H, NQ, 128)).astype(np.float32),
    }


def reference(qT, kT, t, v, gn, og):
    a = np.repeat(mxq(f64(kT), 1, "e4m3"), H // KV, 0).transpose(0, 2, 1) @ mxq(f64(qT), 1, "e4m3")
    p = np.tanh(a)
    w = p * f64(t)
    y = mxq(w, 1, "e4m3").transpose(0, 2, 1) @ np.repeat(mxq(f64(v), 1, "e4m3"), H // KV, 0)
    y = y / 16.0
    y = y / np.sqrt(np.mean(np.square(y), -1, keepdims=True) + 1e-5) * f64(gn)[:1]
    y = y / (1.0 + np.exp(-f64(og)))
    return y

@@ -1,0 +1,396 @@
+from contextlib import ExitStack
+
+import concourse.mybir as mybir
+
+H, KV, D, NQ, N, E = 4, 2, 256, 512, 512, 128
+FLOPS = 2 * H * NQ * N * (D + E)
+
+F32 = mybir.dt.float32
+BF16 = mybir.dt.bfloat16
+U32 = mybir.dt.uint32
+U8 = mybir.dt.uint8
+FP8X4 = mybir.dt.float8_e4m3fn_x4
+ACT = mybir.ActivationFunctionType
+ALU = mybir.AluOpType
+
+P = 128
+ROWS = 64
+PACK = 4
+HALF = 256
+PAIRS = ((1, 2), (0, 3))
+
+STEPS = [
+    ("warm",),
+    ("load_k", 0, 512,),
+    ("load_q", 0,),
+    ("k_deal", "v", 0, 128, 1, 2,),
+    ("k_deal", "v", 0, 128, 3, 4,),
+    ("k_deal", "s", 0, 128, 2, 3,),
+    ("k_quant", 1, 2,),
+    ("load_q", 1,),
+    ("k_quant", 2, 3,),
+    ("k_deal", "s", 0, 128, 0, 1,),
+    ("load_v",),
+    ("q_deal", "v", 0, 0, 1,),
+    ("load_t",),
+    ("q_deal", "s", 0, 1, 2,),
+    ("k_quant", 0, 1,),
+    ("q_quant", 0, 0, 1,),
+    ("q_deal", "s", 1, 1, 2,),
+    ("k_quant", 3, 4,),
+    ("load_q", 2,),
+    ("load_q", 3,),
+    ("q_quant", 0, 1, 2,),
+    ("q_deal", "v", 1, 0, 1,),
+    ("q_quant", 1, 0, 1,),
+    ("scores", 0,),
+    ("tanh", 0, 0,),
+    ("scores", 1,),
+    ("tanh", 0, 1,),
+    ("tanh", 1, 0,),
+    ("scores", 2,),
+    ("tanh", 1, 1,),
+    ("load_gn",),
+    ("q_quant", 1, 1, 2,),
+    ("v_deal", "v", 0,),
+    ("weigh", 0, 0, 1,),
+    ("scores", 3,),
+    ("tanh", 2, 0,),
+    ("v_deal", "v", 1,),
+    ("tanh", 2, 1,),
+    ("w_quant", 0, 0, 1,),
+    ("q_deal", "s", 2, 0, 1,),
+    ("weigh", 0, 1, 2,),
+    ("v_quant",),
+    ("tanh", 3, 1,),
+    ("tanh", 3, 0,),
+    ("load_og", 1,),
+    ("q_deal", "s", 3, 1, 2,),
+    ("w_quant", 0, 1, 2,),
+    ("q_deal", "v", 2, 1, 2,),
+    ("load_og", 3,),
+    ("values", 0, 0,),
+    ("weigh", 1, 0, 2,),
+    ("values", 0, 1,),
+    ("q_quant", 2, 0, 2,),
+    ("w_quant", 1, 0, 2,),
+    ("scores", 4,),
+    ("square", 0, 2,),
+    ("weigh", 2, 0, 2,),
+    ("q_deal", "v", 3, 0, 1,),
+    ("scores", 5,),
+    ("load_og", 0,),
+    ("weigh", 3, 0, 2,),
+    ("square", 0, 0,),
+    ("sigmoid", 1,),
+    ("q_quant", 3, 0, 2,),
+    ("tanh", 5, 0,),
+    ("w_quant", 2, 0, 2,),
+    ("values", 1, 0,),
+    ("w_quant", 3, 0, 2,),
+    ("tanh", 5, 1,),
+    ("values", 1, 1,),
+    ("scores", 7,),
+    ("tanh", 4, 0,),
+    ("gain", 1,),
+    ("weigh", 5, 0, 2,),
+    ("tanh", 4, 1,),
+    ("load_og", 2,),
+    ("weigh", 4, 0, 2,),
+    ("sigmoid", 0,),
+    ("tanh", 7, 1,),
+    ("sigmoid", 2,),
+    ("tanh", 7, 0,),
+    ("scores", 6,),
+    ("weigh", 7, 1, 2,),
+    ("values", 3, 1,),
+    ("w_quant", 4, 0, 2,),
+    ("sigmoid", 3,),
+    ("square", 0, 1,),
+    ("weigh", 7, 0, 1,),
+    ("w_quant", 7, 1, 2,),
+    ("w_quant", 5, 0, 2,),
+    ("values", 3, 0,),
+    ("values", 2, 0,),
+    ("tanh", 6, 0,),
+    ("values", 4, 1,),
+    ("tanh", 6, 1,),
+    ("w_quant", 7, 0, 1,),
+    ("square", 0, 3,),
+    ("values", 2, 1,),
+    ("values", 4, 0,),
+    ("values", 5, 0,),
+    ("square", 1, 3,),
+    ("values", 5, 1,),
+    ("root", 0, 4,),
+    ("square", 1, 1,),
+    ("square", 1, 2,),
+    ("gain", 3,),
+    ("weigh", 6, 0, 2,),
+    ("square", 1, 0,),
+    ("square", 2, 2,),
+    ("square", 2, 3,),
+    ("root", 4, 8,),
+    ("gain", 0,),
+    ("square", 2, 0,),
+    ("w_quant", 6, 0, 2,),
+    ("invert", 0, 4,),
+    ("values", 7, 1,),
+    ("square", 2, 1,),
+    ("values", 6, 0,),
+    ("gain", 2,),
+    ("finish", 0, 1,),
+    ("values", 6, 1,),
+    ("finish", 0, 0,),
+    ("invert", 4, 8,),
+    ("root", 8, 12,),
+    ("finish", 0, 3,),
+    ("finish", 0, 2,),
+    ("values", 7, 0,),
+    ("finish", 1, 0,),
+    ("square", 3, 0,),
+    ("finish", 1, 2,),
+    ("store", 0, 1, 2,),
+    ("invert", 8, 12,),
+    ("finish", 1, 1,),
+    ("square", 3, 2,),
+    ("finish", 1, 3,),
+    ("square", 3, 1,),
+    ("finish", 2, 0,),
+    ("store", 0, 0, 1,),
+    ("square", 3, 3,),
+    ("store", 1, 0, 1,),
+    ("finish", 2, 2,),
+    ("finish", 2, 1,),
+    ("root", 12, 14,),
+    ("store", 1, 1, 2,),
+    ("root", 14, 16,),
+    ("invert", 12, 14,),
+    ("finish", 2, 3,),
+    ("invert", 14, 16,),
+    ("finish", 3, 0,),
+    ("finish", 3, 1,),
+    ("store", 2, 0, 1,),
+    ("finish", 3, 3,),
+    ("store", 2, 1, 2,),
+    ("finish", 3, 2,),
+    ("store", 3, 0, 1,),
+    ("store", 3, 1, 2,),
+]
+
+
+def tile_rows_a_tanh_onorm_gate_kernel(tc, qT, kT, t, v, gn, og, out):
+    nc = tc.nc
+    with ExitStack() as ctx:
+        sb = ctx.enter_context(tc.tile_pool(name="sb", bufs=1))
+        ps = ctx.enter_context(tc.psum_pool(name="ps", bufs=1))
+        ctx.enter_context(tc.manual_schedule())
+
+        def tile(name, shape, dtype):
+            return sb.tile(shape, dtype, name=name, align_bytes=64)
+
+        k_raw = tile("k_raw", [P, PACK, N], F32)
+        k_bf = tile("k_bf", [P, PACK, P, PACK], BF16)
+        k_codes = tile("k_codes", [P, N], U32)
+        k_scales = tile("k_scales", [P, N], U8)
+        q_raw = [tile("q_raw%d" % i, [P, PACK, HALF], F32) for i in range(4)]
+        q_bf = [tile("q_bf%d" % i, [P, 2, P, PACK], BF16) for i in range(4)]
+        q_codes = [tile("q_codes%d" % i, [P, HALF], U32) for i in range(4)]
+        q_scales = [tile("q_scales%d" % i, [P, HALF], U8) for i in range(4)]
+        v_raw = tile("v_raw", [P, KV, PACK, E], F32)
+        v_bf = tile("v_bf", [P, KV, E, PACK], BF16)
+        v_codes = tile("v_codes", [P, KV * E], U32)
+        v_scales = tile("v_scales", [P, KV * E], U8)
+        t_sb = tile("t_sb", [P, 1, PACK], F32)
+        gn_sb = tile("gn_sb", [P, 1, E], F32)
+        og_sb = [tile("og_sb%d" % i, [P, KV, 2 * E], F32) for i in range(4)]
+        sig = [tile("sig%d" % i, [P, 4, E], F32) for i in range(4)]
+        gate = [tile("gate%d" % i, [P, 4, E], F32) for i in range(4)]
+        gated = [tile("gated%d" % i, [P, 4, E], F32) for i in range(4)]
+        res = [tile("res%d" % i, [P, KV, 2 * E], F32) for i in range(4)]
+        p_sb = [tile("p_sb%d" % k, [P, KV, P, PACK], F32) for k in range(8)]
+        w_bf = [tile("w_bf%d" % k, [P, KV * P, PACK], BF16) for k in range(8)]
+        w_codes = [tile("w_codes%d" % k, [P, KV * P], U32) for k in range(8)]
+        w_scales = [tile("w_scales%d" % k, [P, KV * P], U8) for k in range(8)]
+        squares = tile("squares", [P, 16, E], BF16)
+        ssq = tile("ssq", [P, 16], F32)
+        rms = tile("rms", [P, 16], F32)
+        rinv = tile("rinv", [P, 16], F32)
+        warm_in = tile("warm_in", [P, 1], F32)
+        warm_out = tile("warm_out", [P, 1], F32)
+        s_ps = [[ps.tile([P, PACK, P], F32, name="s_ps%d%d" % (g, b)) for b in range(2)] for g in range(KV)]
+        y_ps = [ps.tile([P, 4, E], F32, name="y_ps%d" % i) for i in range(4)]
+
+        def copy_on(eng, dst, src):
+            if eng == "v":
+                nc.vector.tensor_copy(out=dst, in_=src)
+            else:
+                nc.scalar.copy(out=dst, in_=src)
+
+        def quant(codes, scales, src):
+            nc.vector.quantize_mx(out=codes.bitcast(FP8X4), scales=scales, in_=src)
+
+        def load_q(i):
+            pair, u = divmod(i, 2)
+            cols = slice(u * HALF, (u + 1) * HALF)
+            h0, h1 = PAIRS[pair]
+            if h1 == h0 + 1:
+                src = qT[h0 : h0 + 2].rearrange("h (p j) n -> (h p) j n", j=PACK)
+                nc.sync.dma_start(out=q_raw[i][:], in_=src[:, :, cols])
+            else:
+                for g in range(KV):
+                    src = qT[PAIRS[pair][g]].rearrange("(p j) n -> p j n", j=PACK)
+                    nc.sync.dma_start(out=q_raw[i][g * ROWS : (g + 1) * ROWS], in_=src[:, :, cols])
+
+        def rows_of(x, i):
+            pair, u = divmod(i, 2)
+            h0, h1 = PAIRS[pair]
+            return x[h0 : h1 + 1 : h1 - h0].rearrange("h (u m c) e -> u m h (c e)", u=2, c=2)[u]
+
+        def load_og(i):
+            nc.sync.dma_start(out=og_sb[i][:], in_=rows_of(og, i))
+
+        def load_k(n0, n1):
+            src = kT.rearrange("g (p j) n -> (g p) j n", j=PACK)
+            nc.sync.dma_start(out=k_raw[:, :, n0:n1], in_=src[:, :, n0:n1])
+
+        def load_t():
+            nc.sync.dma_start(out=t_sb[:, 0, :], in_=t.rearrange("(p j) o -> p (j o)", j=PACK))
+
+        def load_gn():
+            nc.sync.dma_start(out=gn_sb[:, 0, :], in_=gn)
+
+        def load_v():
+            nc.sync.dma_start(
+                out=v_raw[:].rearrange("p g j e -> p g (j e)"), in_=v.rearrange("g (p j) e -> p g (j e)", j=PACK)
+            )
+
+        def warm():
+            nc.vector.memset(warm_in[:], 0.0)
+            nc.scalar.activation(out=warm_out[:], in_=warm_in[:], func=ACT.Sigmoid)
+
+        def k_deal(eng, s0, s1, r0, r1):
+            dst = k_bf[:, r0:r1, s0:s1, :].rearrange("p r s j -> p s j r")
+            src = k_raw[:].rearrange("p j (s r) -> p s j r", r=PACK)[:, s0:s1, :, r0:r1]
+            copy_on(eng, dst, src)
+
+        def k_quant(r0, r1):
+            cols = slice(r0 * P, r1 * P)
+            quant(k_codes[:, cols], k_scales[:, cols], k_bf[:, r0:r1].rearrange("p r s j -> p (r s j)"))
+
+        def q_deal(eng, i, c0, c1):
+            dst = q_bf[i][:, c0:c1].rearrange("p c m j -> p m j c")
+            src = q_raw[i][:].rearrange("p j (m c) -> p m j c", c=2)[:, :, :, c0:c1]
+            copy_on(eng, dst, src)
+
+        def q_quant(i, c0, c1):
+            cols = slice(c0 * P, c1 * P)
+            quant(q_codes[i][:, cols], q_scales[i][:, cols], q_bf[i][:, c0:c1].rearrange("p c m j -> p (c m j)"))
+
+        def v_deal(eng, g):
+            dst = v_bf[:, g].rearrange("p (a b) j -> p a j b", b=4)
+            src = v_raw[:, g].rearrange("p j (a b) -> p a j b", b=4)
+            copy_on(eng, dst, src)
+
+        def v_quant():
+            quant(v_codes[:], v_scales[:], v_bf[:].rearrange("p g e j -> p (g e j)"))
+
+        def scores(k):
+            i, c = divmod(k, 2)
+            qc = slice(c * P, (c + 1) * P)
+            for r in range(PACK):
+                kc = slice(r * P, (r + 1) * P)
+                for g in range(KV):
+                    rows = slice(g * ROWS, (g + 1) * ROWS)
+                    nc.tensor.matmul_mx(
+                        out=s_ps[g][k % 2][:, r, :],
+                        lhsT=k_codes[rows, kc].bitcast(FP8X4),
+                        lhsT_scale=k_scales[rows, kc],
+                        rhs=q_codes[i][rows, qc].bitcast(FP8X4),
+                        rhs_scale=q_scales[i][rows, qc],
+                        start=True,
+                        stop=True,
+                    )
+
+        def tanh(k, g):
+            nc.scalar.activation(out=p_sb[k][:, g], in_=s_ps[g][k % 2][:].rearrange("p r n -> p n r"), func=ACT.Tanh)
+
+        def weigh(k, g0, g1):
+            n = (g1 - g0) * P
+            nc.vector.tensor_tensor(
+                out=w_bf[k][:, g0 * P : g1 * P, :],
+                in0=p_sb[k][:, g0:g1].rearrange("p g n r -> p (g n) r"),
+                in1=t_sb[:].to_broadcast([P, n, PACK]),
+                op=ALU.mult,
+            )
+
+        def w_quant(k, g0, g1):
+            cols = slice(g0 * P, g1 * P)
+            quant(w_codes[k][:, cols], w_scales[k][:, cols], w_bf[k][:, cols, :].rearrange("p n r -> p (n r)"))
+
+        def values(k, g):
+            i, c = divmod(k, 2)
+            cols = slice(g * P, (g + 1) * P)
+            nc.tensor.matmul_mx(
+                out=y_ps[i][:, 2 * g + c, :],
+                lhsT=w_codes[k][:, cols].bitcast(FP8X4),
+                lhsT_scale=w_scales[k][:, cols],
+                rhs=v_codes[:, cols].bitcast(FP8X4),
+                rhs_scale=v_scales[:, cols],
+                start=True,
+                stop=True,
+            )
+
+        def sigmoid(i):
+            nc.scalar.activation(
+                out=sig[i][:].rearrange("p x e -> p (x e)"), in_=og_sb[i][:].rearrange("p g x -> p (g x)"), func=ACT.Sigmoid
+            )
+
+        def gain(i):
+            nc.vector.tensor_tensor(out=gate[i][:], in0=sig[i][:], in1=gn_sb[:].to_broadcast([P, 4, E]), op=ALU.mult)
+
+        def square(i, x):
+            nc.scalar.activation(
+                out=squares[:, 4 * i + x], in_=y_ps[i][:, x, :], func=ACT.Square, accum_out=ssq[:, 4 * i + x : 4 * i + x + 1]
+            )
+
+        def root(a, b):
+            nc.scalar.activation(out=rms[:, a:b], in_=ssq[:, a:b], func=ACT.Sqrt, scale=1.0 / E, bias=256.0 * 1e-5)
+
+        def invert(a, b):
+            nc.vector.reciprocal(out=rinv[:, a:b], in_=rms[:, a:b])
+
+        def finish(i, x):
+            g, c = divmod(x, 2)
+            nc.vector.scalar_tensor_tensor(
+                out=res[i][:, g, c * E : (c + 1) * E],
+                in0=y_ps[i][:, x, :],
+                scalar=rinv[:, 4 * i + x : 4 * i + x + 1],
+                in1=gate[i][:, x],
+                op0=ALU.mult,
+                op1=ALU.mult,
+            )
+
+        def premul(i, x0, x1):
+            nc.vector.tensor_tensor(out=gated[i][:, x0:x1], in0=y_ps[i][:, x0:x1, :], in1=gate[i][:, x0:x1], op=ALU.mult)
+
+        def scale(i, x):
+            g, c = divmod(x, 2)
+            nc.scalar.activation(
+                out=res[i][:, g, c * E : (c + 1) * E], in_=gated[i][:, x], func=ACT.Copy, scale=rinv[:, 4 * i + x : 4 * i + x + 1]
+            )
+
+        def rsqrt(a, b):
+            nc.scalar.activation(out=rinv[:, a:b], in_=ssq[:, a:b], func=ACT.Abs_reciprocal_sqrt, scale=1.0 / E, bias=256.0 * 1e-5)
+
+        def store(i, g0, g1):
+            nc.sync.dma_start(out=rows_of(out, i)[:, g0:g1], in_=res[i][:, g0:g1])
+
+        do = dict(
+            load_q=load_q, load_og=load_og, load_k=load_k, load_t=load_t, load_gn=load_gn, load_v=load_v, warm=warm,
+            k_deal=k_deal, k_quant=k_quant, q_deal=q_deal, q_quant=q_quant, v_deal=v_deal, v_quant=v_quant,
+            scores=scores, tanh=tanh, weigh=weigh, w_quant=w_quant, values=values, sigmoid=sigmoid, gain=gain,
+            square=square, root=root, invert=invert, finish=finish, store=store, premul=premul, scale=scale, rsqrt=rsqrt,
+        )
+        for step in STEPS:
+            do[step[0]](*step[1:])

@@ -21,161 +21,167 @@ PAIRS = ((1, 2), (0, 3))
 
 STEPS = [
     ("warm",),
-    ("load_k", 0, 512,),
-    ("load_q", 0,),
-    ("k_deal", "v", 0, 128, 1, 2,),
-    ("k_deal", "v", 0, 128, 3, 4,),
-    ("k_deal", "s", 0, 128, 2, 3,),
-    ("k_quant", 1, 2,),
-    ("load_q", 1,),
-    ("k_quant", 2, 3,),
-    ("k_deal", "s", 0, 128, 0, 1,),
-    ("load_v",),
-    ("q_deal", "v", 0, 0, 1,),
-    ("load_t",),
-    ("q_deal", "s", 0, 1, 2,),
+    ("load_k", 0,),
+    ("k_deal", "v", 0, 0, 2,),
+    ("k_deal", "s", 0, 2, 4,),
+    ("k_quant", 0, 0,),
+    ("load_k", 1,),
+    ("k_quant", 0, 3,),
+    ("load_q_first", 1,),
     ("k_quant", 0, 1,),
-    ("q_quant", 0, 0, 1,),
-    ("q_deal", "s", 1, 1, 2,),
-    ("k_quant", 3, 4,),
+    ("k_deal", "v", 1, 2, 4,),
+    ("k_quant", 0, 2,),
+    ("k_deal", "s", 1, 0, 2,),
+    ("load_q_first", 0,),
+    ("load_q", 1,),
+    ("k_quant", 1, 3,),
+    ("q_first_deal", "v", 1,),
+    ("load_t",),
+    ("k_quant", 1, 0,),
+    ("k_quant", 1, 1,),
     ("load_q", 2,),
-    ("load_q", 3,),
     ("q_quant", 0, 1, 2,),
-    ("q_deal", "v", 1, 0, 1,),
-    ("q_quant", 1, 0, 1,),
-    ("scores", 0,),
-    ("tanh", 0, 0,),
-    ("scores", 1,),
-    ("tanh", 0, 1,),
+    ("k_quant", 1, 2,),
+    ("scores", 1, 0,),
+    ("scores", 1, 1,),
     ("tanh", 1, 0,),
-    ("scores", 2,),
+    ("q_first_deal", "v", 0,),
+    ("q_quant", 0, 0, 1,),
+    ("scores", 0, 0,),
+    ("scores", 0, 1,),
+    ("q_deal", "v", 1, 0, 64,),
     ("tanh", 1, 1,),
+    ("tanh", 0, 1,),
+    ("tanh", 0, 0,),
+    ("load_q", 3,),
+    ("q_quant", 1, 0, 2,),
     ("load_gn",),
-    ("q_quant", 1, 1, 2,),
-    ("v_deal", "v", 0,),
-    ("weigh", 0, 0, 1,),
-    ("scores", 3,),
-    ("tanh", 2, 0,),
-    ("v_deal", "v", 1,),
-    ("tanh", 2, 1,),
-    ("w_quant", 0, 0, 1,),
-    ("q_deal", "s", 2, 0, 1,),
-    ("weigh", 0, 1, 2,),
-    ("v_quant",),
-    ("tanh", 3, 1,),
-    ("tanh", 3, 0,),
-    ("load_og", 1,),
-    ("q_deal", "s", 3, 1, 2,),
-    ("w_quant", 0, 1, 2,),
-    ("q_deal", "v", 2, 1, 2,),
-    ("load_og", 3,),
-    ("values", 0, 0,),
+    ("scores", 3, 0,),
+    ("scores", 3, 1,),
     ("weigh", 1, 0, 2,),
-    ("values", 0, 1,),
-    ("q_quant", 2, 0, 2,),
+    ("tanh", 3, 0,),
+    ("scores", 2, 1,),
+    ("weigh", 0, 1, 2,),
+    ("scores", 2, 0,),
+    ("q_deal", "s", 2, 0, 32,),
     ("w_quant", 1, 0, 2,),
-    ("scores", 4,),
-    ("square", 0, 2,),
-    ("weigh", 2, 0, 2,),
-    ("q_deal", "v", 3, 0, 1,),
-    ("scores", 5,),
-    ("load_og", 0,),
+    ("tanh", 3, 1,),
+    ("weigh", 0, 0, 1,),
+    ("load_v",),
+    ("tanh", 2, 0,),
+    ("q_deal", "v", 2, 32, 64,),
+    ("w_quant", 0, 0, 1,),
+    ("w_quant", 0, 1, 2,),
+    ("q_quant", 2, 0, 2,),
+    ("tanh", 2, 1,),
     ("weigh", 3, 0, 2,),
-    ("square", 0, 0,),
-    ("sigmoid", 1,),
+    ("weigh", 2, 0, 2,),
+    ("q_deal", "s", 3, 0, 64,),
+    ("scores", 5, 1,),
+    ("scores", 4, 0,),
     ("q_quant", 3, 0, 2,),
-    ("tanh", 5, 0,),
-    ("w_quant", 2, 0, 2,),
-    ("values", 1, 0,),
-    ("w_quant", 3, 0, 2,),
-    ("tanh", 5, 1,),
-    ("values", 1, 1,),
-    ("scores", 7,),
+    ("scores", 5, 0,),
+    ("load_og", 0,),
     ("tanh", 4, 0,),
-    ("gain", 1,),
+    ("v_deal", "v", 0,),
+    ("tanh", 5, 1,),
+    ("scores", 4, 1,),
+    ("tanh", 5, 0,),
+    ("v_deal", "v", 1,),
+    ("w_quant", 3, 0, 2,),
+    ("scores", 6, 0,),
+    ("scores", 7, 1,),
+    ("v_quant",),
     ("weigh", 5, 0, 2,),
     ("tanh", 4, 1,),
-    ("load_og", 2,),
-    ("weigh", 4, 0, 2,),
-    ("sigmoid", 0,),
-    ("tanh", 7, 1,),
-    ("sigmoid", 2,),
-    ("tanh", 7, 0,),
-    ("scores", 6,),
-    ("weigh", 7, 1, 2,),
-    ("values", 3, 1,),
-    ("w_quant", 4, 0, 2,),
-    ("sigmoid", 3,),
-    ("square", 0, 1,),
-    ("weigh", 7, 0, 1,),
-    ("w_quant", 7, 1, 2,),
-    ("w_quant", 5, 0, 2,),
+    ("w_quant", 2, 0, 2,),
+    ("scores", 7, 0,),
+    ("scores", 6, 1,),
     ("values", 3, 0,),
-    ("values", 2, 0,),
     ("tanh", 6, 0,),
-    ("values", 4, 1,),
+    ("w_quant", 5, 0, 2,),
+    ("tanh", 7, 1,),
+    ("tanh", 7, 0,),
+    ("load_og", 3,),
+    ("values", 1, 1,),
+    ("values", 1, 0,),
+    ("weigh", 4, 0, 2,),
+    ("weigh", 7, 1, 2,),
+    ("values", 0, 1,),
     ("tanh", 6, 1,),
-    ("w_quant", 7, 0, 1,),
-    ("square", 0, 3,),
-    ("values", 2, 1,),
-    ("values", 4, 0,),
-    ("values", 5, 0,),
-    ("square", 1, 3,),
-    ("values", 5, 1,),
-    ("root", 0, 4,),
-    ("square", 1, 1,),
-    ("square", 1, 2,),
-    ("gain", 3,),
     ("weigh", 6, 0, 2,),
-    ("square", 1, 0,),
-    ("square", 2, 2,),
-    ("square", 2, 3,),
-    ("root", 4, 8,),
-    ("gain", 0,),
-    ("square", 2, 0,),
+    ("w_quant", 4, 0, 2,),
+    ("w_quant", 7, 1, 2,),
+    ("sigmoid", 3,),
+    ("values", 0, 0,),
+    ("square", 0, 2,),
+    ("load_og", 2,),
+    ("values", 3, 1,),
+    ("values", 2, 1,),
+    ("square", 0, 3,),
     ("w_quant", 6, 0, 2,),
-    ("invert", 0, 4,),
+    ("square", 0, 0,),
+    ("weigh", 7, 0, 1,),
+    ("load_og", 1,),
+    ("values", 5, 1,),
+    ("sigmoid", 0,),
+    ("sigmoid", 2,),
+    ("sigmoid", 1,),
+    ("values", 4, 1,),
+    ("square", 0, 1,),
+    ("values", 5, 0,),
+    ("values", 4, 0,),
+    ("gain", 3,),
+    ("w_quant", 7, 0, 1,),
+    ("rsqrt", 0, 4,),
+    ("gain", 0,),
     ("values", 7, 1,),
     ("square", 2, 1,),
-    ("values", 6, 0,),
     ("gain", 2,),
-    ("finish", 0, 1,),
-    ("values", 6, 1,),
     ("finish", 0, 0,),
-    ("invert", 4, 8,),
-    ("root", 8, 12,),
-    ("finish", 0, 3,),
+    ("values", 6, 0,),
+    ("values", 6, 1,),
     ("finish", 0, 2,),
+    ("square", 2, 3,),
+    ("square", 2, 2,),
     ("values", 7, 0,),
-    ("finish", 1, 0,),
-    ("square", 3, 0,),
-    ("finish", 1, 2,),
-    ("store", 0, 1, 2,),
-    ("invert", 8, 12,),
-    ("finish", 1, 1,),
-    ("square", 3, 2,),
-    ("finish", 1, 3,),
+    ("finish", 0, 3,),
+    ("values", 2, 0,),
+    ("square", 2, 0,),
+    ("square", 1, 0,),
     ("square", 3, 1,),
-    ("finish", 2, 0,),
+    ("finish", 0, 1,),
+    ("gain", 1,),
+    ("rsqrt", 8, 12,),
+    ("square", 3, 0,),
     ("store", 0, 0, 1,),
     ("square", 3, 3,),
-    ("store", 1, 0, 1,),
+    ("store", 0, 1, 2,),
+    ("square", 3, 2,),
+    ("rsqrt", 12, 14,),
     ("finish", 2, 2,),
-    ("finish", 2, 1,),
-    ("root", 12, 14,),
-    ("store", 1, 1, 2,),
-    ("root", 14, 16,),
-    ("invert", 12, 14,),
+    ("square", 1, 1,),
     ("finish", 2, 3,),
-    ("invert", 14, 16,),
+    ("finish", 2, 0,),
+    ("finish", 2, 1,),
+    ("rsqrt", 14, 16,),
+    ("square", 1, 3,),
+    ("store", 2, 1, 2,),
     ("finish", 3, 0,),
     ("finish", 3, 1,),
     ("store", 2, 0, 1,),
-    ("finish", 3, 3,),
-    ("store", 2, 1, 2,),
     ("finish", 3, 2,),
+    ("square", 1, 2,),
     ("store", 3, 0, 1,),
+    ("premul", 1, 0, 2,),
+    ("rsqrt", 4, 8,),
+    ("scale", 1, 0,),
+    ("scale", 1, 1,),
+    ("finish", 3, 3,),
+    ("finish", 1, 3,),
+    ("finish", 1, 2,),
     ("store", 3, 1, 2,),
+    ("store", 1, 0, 2,),
 ]
 
 
@@ -189,11 +195,12 @@ def tile_rows_a_tanh_onorm_gate_kernel(tc, qT, kT, t, v, gn, og, out):
         def tile(name, shape, dtype):
             return sb.tile(shape, dtype, name=name, align_bytes=64)
 
-        k_raw = tile("k_raw", [P, PACK, N], F32)
-        k_bf = tile("k_bf", [P, PACK, P, PACK], BF16)
+        k_raw = [tile("k_raw%d" % w, [P, PACK, HALF], F32) for w in range(2)]
+        k_bf = [tile("k_bf%d" % w, [P, PACK, ROWS, PACK], BF16) for w in range(2)]
+        q_first = [tile("q_first%d" % c, [P, PACK, P], F32) for c in range(2)]
         k_codes = tile("k_codes", [P, N], U32)
         k_scales = tile("k_scales", [P, N], U8)
-        q_raw = [tile("q_raw%d" % i, [P, PACK, HALF], F32) for i in range(4)]
+        q_raw = {i: tile("q_raw%d" % i, [P, PACK, HALF], F32) for i in range(1, 4)}
         q_bf = [tile("q_bf%d" % i, [P, 2, P, PACK], BF16) for i in range(4)]
         q_codes = [tile("q_codes%d" % i, [P, HALF], U32) for i in range(4)]
         q_scales = [tile("q_scales%d" % i, [P, HALF], U8) for i in range(4)]
@@ -216,6 +223,7 @@ def tile_rows_a_tanh_onorm_gate_kernel(tc, qT, kT, t, v, gn, og, out):
         ssq = tile("ssq", [P, 16], F32)
         rms = tile("rms", [P, 16], F32)
         rinv = tile("rinv", [P, 16], F32)
+        expo = tile("expo", [P, 16], F32)
         warm_in = tile("warm_in", [P, 1], F32)
         warm_out = tile("warm_out", [P, 1], F32)
         s_ps = [[ps.tile([P, PACK, P], F32, name="s_ps%d%d" % (g, b)) for b in range(2)] for g in range(KV)]
@@ -229,6 +237,11 @@ def tile_rows_a_tanh_onorm_gate_kernel(tc, qT, kT, t, v, gn, og, out):
 
         def quant(codes, scales, src):
             nc.vector.quantize_mx(out=codes.bitcast(FP8X4), scales=scales, in_=src)
+
+        def load_q_first(c):
+            h0 = PAIRS[0][0]
+            src = qT[h0 : h0 + 2].rearrange("h (p j) n -> (h p) j n", j=PACK)
+            nc.sync.dma_start(out=q_first[c][:], in_=src[:, :, c * P : (c + 1) * P])
 
         def load_q(i):
             pair, u = divmod(i, 2)
@@ -247,12 +260,19 @@ def tile_rows_a_tanh_onorm_gate_kernel(tc, qT, kT, t, v, gn, og, out):
             h0, h1 = PAIRS[pair]
             return x[h0 : h1 + 1 : h1 - h0].rearrange("h (u m c) e -> u m h (c e)", u=2, c=2)[u]
 
-        def load_og(i):
-            nc.sync.dma_start(out=og_sb[i][:], in_=rows_of(og, i))
+        def plain_rows(x, g):
+            return x[PAIRS[0][g], :HALF].rearrange("(c m) e -> m c e", c=2)
 
-        def load_k(n0, n1):
+        def load_og(i):
+            if i == 0:
+                for g in range(KV):
+                    nc.sync.dma_start(out=og_sb[0][:, g].rearrange("p (c e) -> p c e", c=2), in_=plain_rows(og, g))
+            else:
+                nc.sync.dma_start(out=og_sb[i][:], in_=rows_of(og, i))
+
+        def load_k(w):
             src = kT.rearrange("g (p j) n -> (g p) j n", j=PACK)
-            nc.sync.dma_start(out=k_raw[:, :, n0:n1], in_=src[:, :, n0:n1])
+            nc.sync.dma_start(out=k_raw[w][:], in_=src[:, :, w * HALF : (w + 1) * HALF])
 
         def load_t():
             nc.sync.dma_start(out=t_sb[:, 0, :], in_=t.rearrange("(p j) o -> p (j o)", j=PACK))
@@ -269,18 +289,23 @@ def tile_rows_a_tanh_onorm_gate_kernel(tc, qT, kT, t, v, gn, og, out):
             nc.vector.memset(warm_in[:], 0.0)
             nc.scalar.activation(out=warm_out[:], in_=warm_in[:], func=ACT.Sigmoid)
 
-        def k_deal(eng, s0, s1, r0, r1):
-            dst = k_bf[:, r0:r1, s0:s1, :].rearrange("p r s j -> p s j r")
-            src = k_raw[:].rearrange("p j (s r) -> p s j r", r=PACK)[:, s0:s1, :, r0:r1]
+        def k_deal(eng, w, r0, r1):
+            dst = k_bf[w][:, r0:r1].rearrange("p r s j -> p s j r")
+            src = k_raw[w][:].rearrange("p j (s r) -> p s j r", r=PACK)[:, :, :, r0:r1]
             copy_on(eng, dst, src)
 
-        def k_quant(r0, r1):
-            cols = slice(r0 * P, r1 * P)
-            quant(k_codes[:, cols], k_scales[:, cols], k_bf[:, r0:r1].rearrange("p r s j -> p (r s j)"))
+        def k_quant(w, r):
+            cols = slice(r * P + w * ROWS, r * P + (w + 1) * ROWS)
+            quant(k_codes[:, cols], k_scales[:, cols], k_bf[w][:, r].rearrange("p s j -> p (s j)"))
 
-        def q_deal(eng, i, c0, c1):
-            dst = q_bf[i][:, c0:c1].rearrange("p c m j -> p m j c")
-            src = q_raw[i][:].rearrange("p j (m c) -> p m j c", c=2)[:, :, :, c0:c1]
+        def q_first_deal(eng, c):
+            dst = q_bf[0][:, c].rearrange("p (a b) j -> p a j b", b=4)
+            src = q_first[c][:].rearrange("p j (a b) -> p a j b", b=4)
+            copy_on(eng, dst, src)
+
+        def q_deal(eng, i, a0, a1):
+            dst = q_bf[i][:].rearrange("p c (a b) j -> p a j b c", b=2)[:, a0:a1]
+            src = q_raw[i][:].rearrange("p j (a b c) -> p a j b c", b=2, c=2)[:, a0:a1]
             copy_on(eng, dst, src)
 
         def q_quant(i, c0, c1):
@@ -295,22 +320,21 @@ def tile_rows_a_tanh_onorm_gate_kernel(tc, qT, kT, t, v, gn, og, out):
         def v_quant():
             quant(v_codes[:], v_scales[:], v_bf[:].rearrange("p g e j -> p (g e j)"))
 
-        def scores(k):
+        def scores(k, g):
             i, c = divmod(k, 2)
             qc = slice(c * P, (c + 1) * P)
+            rows = slice(g * ROWS, (g + 1) * ROWS)
             for r in range(PACK):
                 kc = slice(r * P, (r + 1) * P)
-                for g in range(KV):
-                    rows = slice(g * ROWS, (g + 1) * ROWS)
-                    nc.tensor.matmul_mx(
-                        out=s_ps[g][k % 2][:, r, :],
-                        lhsT=k_codes[rows, kc].bitcast(FP8X4),
-                        lhsT_scale=k_scales[rows, kc],
-                        rhs=q_codes[i][rows, qc].bitcast(FP8X4),
-                        rhs_scale=q_scales[i][rows, qc],
-                        start=True,
-                        stop=True,
-                    )
+                nc.tensor.matmul_mx(
+                    out=s_ps[g][k % 2][:, r, :],
+                    lhsT=k_codes[rows, kc].bitcast(FP8X4),
+                    lhsT_scale=k_scales[rows, kc],
+                    rhs=q_codes[i][rows, qc].bitcast(FP8X4),
+                    rhs_scale=q_scales[i][rows, qc],
+                    start=True,
+                    stop=True,
+                )
 
         def tanh(k, g):
             nc.scalar.activation(out=p_sb[k][:, g], in_=s_ps[g][k % 2][:].rearrange("p r n -> p n r"), func=ACT.Tanh)
@@ -383,14 +407,40 @@ def tile_rows_a_tanh_onorm_gate_kernel(tc, qT, kT, t, v, gn, og, out):
         def rsqrt(a, b):
             nc.scalar.activation(out=rinv[:, a:b], in_=ssq[:, a:b], func=ACT.Abs_reciprocal_sqrt, scale=1.0 / E, bias=256.0 * 1e-5)
 
+        def mean(a, b):
+            nc.vector.tensor_scalar(
+                out=rms[:, a:b], in0=ssq[:, a:b], scalar1=1.0 / E, scalar2=256.0 * 1e-5, op0=ALU.mult, op1=ALU.add
+            )
+
+        def power(a, b):
+            nc.gpsimd.tensor_tensor(out=rinv[:, a:b], in0=rms[:, a:b], in1=expo[:, a:b], op=ALU.pow)
+
+        def set_expo():
+            nc.gpsimd.memset(expo[:], -0.5)
+
+        def pgain(i, x0, x1):
+            nc.gpsimd.tensor_tensor(
+                out=gate[i][:, x0:x1], in0=sig[i][:, x0:x1], in1=gn_sb[:].to_broadcast([P, x1 - x0, E]), op=ALU.mult
+            )
+
+        def pscale(i, x):
+            g, c = divmod(x, 2)
+            nc.gpsimd.tensor_scalar(
+                out=res[i][:, g, c * E : (c + 1) * E], in0=gated[i][:, x], scalar1=rinv[:, 4 * i + x : 4 * i + x + 1],
+                scalar2=0.0, op0=ALU.mult, op1=ALU.add,
+            )
+
         def store(i, g0, g1):
-            nc.sync.dma_start(out=rows_of(out, i)[:, g0:g1], in_=res[i][:, g0:g1])
+            if i == 0:
+                nc.sync.dma_start(out=plain_rows(out, g0), in_=res[0][:, g0].rearrange("p (c e) -> p c e", c=2))
+            else:
+                nc.sync.dma_start(out=rows_of(out, i)[:, g0:g1], in_=res[i][:, g0:g1])
 
         do = dict(
             load_q=load_q, load_og=load_og, load_k=load_k, load_t=load_t, load_gn=load_gn, load_v=load_v, warm=warm,
             k_deal=k_deal, k_quant=k_quant, q_deal=q_deal, q_quant=q_quant, v_deal=v_deal, v_quant=v_quant,
             scores=scores, tanh=tanh, weigh=weigh, w_quant=w_quant, values=values, sigmoid=sigmoid, gain=gain,
-            square=square, root=root, invert=invert, finish=finish, store=store, premul=premul, scale=scale, rsqrt=rsqrt,
+            square=square, root=root, invert=invert, finish=finish, store=store, mean=mean, power=power, set_expo=set_expo, pgain=pgain, pscale=pscale, load_q_first=load_q_first, q_first_deal=q_first_deal, premul=premul, scale=scale, rsqrt=rsqrt,
         )
         for step in STEPS:
             do[step[0]](*step[1:])

from contextlib import ExitStack

import concourse.mybir as mybir

H, KV, D, NQ, N, E = 4, 2, 256, 512, 512, 128
FLOPS = 2 * H * NQ * N * (D + E)

F32 = mybir.dt.float32
BF16 = mybir.dt.bfloat16
U32 = mybir.dt.uint32
U8 = mybir.dt.uint8
FP8X4 = mybir.dt.float8_e4m3fn_x4
ACT = mybir.ActivationFunctionType
ALU = mybir.AluOpType

P = 128
ROWS = 64
PACK = 4
HALF = 256
PAIRS = ((1, 2), (0, 3))

STEPS = [
    ("warm",),
    ("load_k", 0,),
    ("k_deal", "v", 0, 0, 2,),
    ("k_deal", "s", 0, 2, 4,),
    ("k_quant", 0, 0,),
    ("load_k", 1,),
    ("k_quant", 0, 3,),
    ("load_q_first", 1,),
    ("k_quant", 0, 1,),
    ("k_deal", "v", 1, 2, 4,),
    ("k_quant", 0, 2,),
    ("k_deal", "s", 1, 0, 2,),
    ("load_q_first", 0,),
    ("load_q", 1,),
    ("k_quant", 1, 3,),
    ("q_first_deal", "v", 1,),
    ("load_t",),
    ("k_quant", 1, 0,),
    ("k_quant", 1, 1,),
    ("load_q", 2,),
    ("q_quant", 0, 1, 2,),
    ("k_quant", 1, 2,),
    ("scores", 1, 0,),
    ("scores", 1, 1,),
    ("tanh", 1, 0,),
    ("q_first_deal", "v", 0,),
    ("q_quant", 0, 0, 1,),
    ("scores", 0, 0,),
    ("scores", 0, 1,),
    ("q_deal", "v", 1, 0, 64,),
    ("tanh", 1, 1,),
    ("tanh", 0, 1,),
    ("tanh", 0, 0,),
    ("load_q", 3,),
    ("q_quant", 1, 0, 2,),
    ("load_gn",),
    ("scores", 3, 0,),
    ("scores", 3, 1,),
    ("weigh", 1, 0, 2,),
    ("tanh", 3, 0,),
    ("scores", 2, 1,),
    ("weigh", 0, 1, 2,),
    ("scores", 2, 0,),
    ("q_deal", "s", 2, 0, 32,),
    ("w_quant", 1, 0, 2,),
    ("tanh", 3, 1,),
    ("weigh", 0, 0, 1,),
    ("load_v",),
    ("tanh", 2, 0,),
    ("q_deal", "v", 2, 32, 64,),
    ("w_quant", 0, 0, 1,),
    ("w_quant", 0, 1, 2,),
    ("q_quant", 2, 0, 2,),
    ("tanh", 2, 1,),
    ("weigh", 3, 0, 2,),
    ("weigh", 2, 0, 2,),
    ("q_deal", "s", 3, 0, 64,),
    ("scores", 5, 1,),
    ("scores", 4, 0,),
    ("q_quant", 3, 0, 2,),
    ("scores", 5, 0,),
    ("load_og", 0,),
    ("tanh", 4, 0,),
    ("v_deal", "v", 0,),
    ("tanh", 5, 1,),
    ("scores", 4, 1,),
    ("tanh", 5, 0,),
    ("v_deal", "v", 1,),
    ("w_quant", 3, 0, 2,),
    ("scores", 6, 0,),
    ("scores", 7, 1,),
    ("v_quant",),
    ("weigh", 5, 0, 2,),
    ("tanh", 4, 1,),
    ("w_quant", 2, 0, 2,),
    ("scores", 7, 0,),
    ("scores", 6, 1,),
    ("values", 3, 0,),
    ("tanh", 6, 0,),
    ("w_quant", 5, 0, 2,),
    ("tanh", 7, 1,),
    ("tanh", 7, 0,),
    ("load_og", 3,),
    ("values", 1, 1,),
    ("values", 1, 0,),
    ("weigh", 4, 0, 2,),
    ("weigh", 7, 1, 2,),
    ("values", 0, 1,),
    ("tanh", 6, 1,),
    ("weigh", 6, 0, 2,),
    ("w_quant", 4, 0, 2,),
    ("w_quant", 7, 1, 2,),
    ("sigmoid", 3,),
    ("values", 0, 0,),
    ("square", 0, 2,),
    ("load_og", 2,),
    ("values", 3, 1,),
    ("values", 2, 1,),
    ("square", 0, 3,),
    ("w_quant", 6, 0, 2,),
    ("square", 0, 0,),
    ("weigh", 7, 0, 1,),
    ("load_og", 1,),
    ("values", 5, 1,),
    ("sigmoid", 0,),
    ("sigmoid", 2,),
    ("sigmoid", 1,),
    ("values", 4, 1,),
    ("square", 0, 1,),
    ("values", 5, 0,),
    ("values", 4, 0,),
    ("gain", 3,),
    ("w_quant", 7, 0, 1,),
    ("rsqrt", 0, 4,),
    ("gain", 0,),
    ("values", 7, 1,),
    ("square", 2, 1,),
    ("gain", 2,),
    ("finish", 0, 0,),
    ("values", 6, 0,),
    ("values", 6, 1,),
    ("finish", 0, 2,),
    ("square", 2, 3,),
    ("square", 2, 2,),
    ("values", 7, 0,),
    ("finish", 0, 3,),
    ("values", 2, 0,),
    ("square", 2, 0,),
    ("square", 1, 0,),
    ("square", 3, 1,),
    ("finish", 0, 1,),
    ("gain", 1,),
    ("rsqrt", 8, 12,),
    ("square", 3, 0,),
    ("store", 0, 0, 1,),
    ("square", 3, 3,),
    ("store", 0, 1, 2,),
    ("square", 3, 2,),
    ("rsqrt", 12, 14,),
    ("finish", 2, 2,),
    ("square", 1, 1,),
    ("finish", 2, 3,),
    ("finish", 2, 0,),
    ("finish", 2, 1,),
    ("rsqrt", 14, 16,),
    ("square", 1, 3,),
    ("store", 2, 1, 2,),
    ("finish", 3, 0,),
    ("finish", 3, 1,),
    ("store", 2, 0, 1,),
    ("finish", 3, 2,),
    ("square", 1, 2,),
    ("store", 3, 0, 1,),
    ("premul", 1, 0, 2,),
    ("rsqrt", 4, 8,),
    ("scale", 1, 0,),
    ("scale", 1, 1,),
    ("finish", 3, 3,),
    ("finish", 1, 3,),
    ("finish", 1, 2,),
    ("store", 3, 1, 2,),
    ("store", 1, 0, 2,),
]


def tile_rows_a_tanh_onorm_gate_kernel(tc, qT, kT, t, v, gn, og, out):
    nc = tc.nc
    with ExitStack() as ctx:
        sb = ctx.enter_context(tc.tile_pool(name="sb", bufs=1))
        ps = ctx.enter_context(tc.psum_pool(name="ps", bufs=1))
        ctx.enter_context(tc.manual_schedule())

        def tile(name, shape, dtype):
            return sb.tile(shape, dtype, name=name, align_bytes=64)

        k_raw = [tile("k_raw%d" % w, [P, PACK, HALF], F32) for w in range(2)]
        k_bf = [tile("k_bf%d" % w, [P, PACK, ROWS, PACK], BF16) for w in range(2)]
        q_first = [tile("q_first%d" % c, [P, PACK, P], F32) for c in range(2)]
        k_codes = tile("k_codes", [P, N], U32)
        k_scales = tile("k_scales", [P, N], U8)
        q_raw = {i: tile("q_raw%d" % i, [P, PACK, HALF], F32) for i in range(1, 4)}
        q_bf = [tile("q_bf%d" % i, [P, 2, P, PACK], BF16) for i in range(4)]
        q_codes = [tile("q_codes%d" % i, [P, HALF], U32) for i in range(4)]
        q_scales = [tile("q_scales%d" % i, [P, HALF], U8) for i in range(4)]
        v_raw = tile("v_raw", [P, KV, PACK, E], F32)
        v_bf = tile("v_bf", [P, KV, E, PACK], BF16)
        v_codes = tile("v_codes", [P, KV * E], U32)
        v_scales = tile("v_scales", [P, KV * E], U8)
        t_sb = tile("t_sb", [P, 1, PACK], F32)
        gn_sb = tile("gn_sb", [P, 1, E], F32)
        og_sb = [tile("og_sb%d" % i, [P, KV, 2 * E], F32) for i in range(4)]
        sig = [tile("sig%d" % i, [P, 4, E], F32) for i in range(4)]
        gate = [tile("gate%d" % i, [P, 4, E], F32) for i in range(4)]
        gated = [tile("gated%d" % i, [P, 4, E], F32) for i in range(4)]
        res = [tile("res%d" % i, [P, KV, 2 * E], F32) for i in range(4)]
        p_sb = [tile("p_sb%d" % k, [P, KV, P, PACK], F32) for k in range(8)]
        w_bf = [tile("w_bf%d" % k, [P, KV * P, PACK], BF16) for k in range(8)]
        w_codes = [tile("w_codes%d" % k, [P, KV * P], U32) for k in range(8)]
        w_scales = [tile("w_scales%d" % k, [P, KV * P], U8) for k in range(8)]
        squares = tile("squares", [P, 16, E], BF16)
        ssq = tile("ssq", [P, 16], F32)
        rms = tile("rms", [P, 16], F32)
        rinv = tile("rinv", [P, 16], F32)
        expo = tile("expo", [P, 16], F32)
        warm_in = tile("warm_in", [P, 1], F32)
        warm_out = tile("warm_out", [P, 1], F32)
        s_ps = [[ps.tile([P, PACK, P], F32, name="s_ps%d%d" % (g, b)) for b in range(2)] for g in range(KV)]
        y_ps = [ps.tile([P, 4, E], F32, name="y_ps%d" % i) for i in range(4)]

        def copy_on(eng, dst, src):
            if eng == "v":
                nc.vector.tensor_copy(out=dst, in_=src)
            else:
                nc.scalar.copy(out=dst, in_=src)

        def quant(codes, scales, src):
            nc.vector.quantize_mx(out=codes.bitcast(FP8X4), scales=scales, in_=src)

        def load_q_first(c):
            h0 = PAIRS[0][0]
            src = qT[h0 : h0 + 2].rearrange("h (p j) n -> (h p) j n", j=PACK)
            nc.sync.dma_start(out=q_first[c][:], in_=src[:, :, c * P : (c + 1) * P])

        def load_q(i):
            pair, u = divmod(i, 2)
            cols = slice(u * HALF, (u + 1) * HALF)
            h0, h1 = PAIRS[pair]
            if h1 == h0 + 1:
                src = qT[h0 : h0 + 2].rearrange("h (p j) n -> (h p) j n", j=PACK)
                nc.sync.dma_start(out=q_raw[i][:], in_=src[:, :, cols])
            else:
                for g in range(KV):
                    src = qT[PAIRS[pair][g]].rearrange("(p j) n -> p j n", j=PACK)
                    nc.sync.dma_start(out=q_raw[i][g * ROWS : (g + 1) * ROWS], in_=src[:, :, cols])

        def rows_of(x, i):
            pair, u = divmod(i, 2)
            h0, h1 = PAIRS[pair]
            return x[h0 : h1 + 1 : h1 - h0].rearrange("h (u m c) e -> u m h (c e)", u=2, c=2)[u]

        def plain_rows(x, g):
            return x[PAIRS[0][g], :HALF].rearrange("(c m) e -> m c e", c=2)

        def load_og(i):
            if i == 0:
                for g in range(KV):
                    nc.sync.dma_start(out=og_sb[0][:, g].rearrange("p (c e) -> p c e", c=2), in_=plain_rows(og, g))
            else:
                nc.sync.dma_start(out=og_sb[i][:], in_=rows_of(og, i))

        def load_k(w):
            src = kT.rearrange("g (p j) n -> (g p) j n", j=PACK)
            nc.sync.dma_start(out=k_raw[w][:], in_=src[:, :, w * HALF : (w + 1) * HALF])

        def load_t():
            nc.sync.dma_start(out=t_sb[:, 0, :], in_=t.rearrange("(p j) o -> p (j o)", j=PACK))

        def load_gn():
            nc.sync.dma_start(out=gn_sb[:, 0, :], in_=gn)

        def load_v():
            nc.sync.dma_start(
                out=v_raw[:].rearrange("p g j e -> p g (j e)"), in_=v.rearrange("g (p j) e -> p g (j e)", j=PACK)
            )

        def warm():
            nc.vector.memset(warm_in[:], 0.0)
            nc.scalar.activation(out=warm_out[:], in_=warm_in[:], func=ACT.Sigmoid)

        def k_deal(eng, w, r0, r1):
            dst = k_bf[w][:, r0:r1].rearrange("p r s j -> p s j r")
            src = k_raw[w][:].rearrange("p j (s r) -> p s j r", r=PACK)[:, :, :, r0:r1]
            copy_on(eng, dst, src)

        def k_quant(w, r):
            cols = slice(r * P + w * ROWS, r * P + (w + 1) * ROWS)
            quant(k_codes[:, cols], k_scales[:, cols], k_bf[w][:, r].rearrange("p s j -> p (s j)"))

        def q_first_deal(eng, c):
            dst = q_bf[0][:, c].rearrange("p (a b) j -> p a j b", b=4)
            src = q_first[c][:].rearrange("p j (a b) -> p a j b", b=4)
            copy_on(eng, dst, src)

        def q_deal(eng, i, a0, a1):
            dst = q_bf[i][:].rearrange("p c (a b) j -> p a j b c", b=2)[:, a0:a1]
            src = q_raw[i][:].rearrange("p j (a b c) -> p a j b c", b=2, c=2)[:, a0:a1]
            copy_on(eng, dst, src)

        def q_quant(i, c0, c1):
            cols = slice(c0 * P, c1 * P)
            quant(q_codes[i][:, cols], q_scales[i][:, cols], q_bf[i][:, c0:c1].rearrange("p c m j -> p (c m j)"))

        def v_deal(eng, g):
            dst = v_bf[:, g].rearrange("p (a b) j -> p a j b", b=4)
            src = v_raw[:, g].rearrange("p j (a b) -> p a j b", b=4)
            copy_on(eng, dst, src)

        def v_quant():
            quant(v_codes[:], v_scales[:], v_bf[:].rearrange("p g e j -> p (g e j)"))

        def scores(k, g):
            i, c = divmod(k, 2)
            qc = slice(c * P, (c + 1) * P)
            rows = slice(g * ROWS, (g + 1) * ROWS)
            for r in range(PACK):
                kc = slice(r * P, (r + 1) * P)
                nc.tensor.matmul_mx(
                    out=s_ps[g][k % 2][:, r, :],
                    lhsT=k_codes[rows, kc].bitcast(FP8X4),
                    lhsT_scale=k_scales[rows, kc],
                    rhs=q_codes[i][rows, qc].bitcast(FP8X4),
                    rhs_scale=q_scales[i][rows, qc],
                    start=True,
                    stop=True,
                )

        def tanh(k, g):
            nc.scalar.activation(out=p_sb[k][:, g], in_=s_ps[g][k % 2][:].rearrange("p r n -> p n r"), func=ACT.Tanh)

        def weigh(k, g0, g1):
            n = (g1 - g0) * P
            nc.vector.tensor_tensor(
                out=w_bf[k][:, g0 * P : g1 * P, :],
                in0=p_sb[k][:, g0:g1].rearrange("p g n r -> p (g n) r"),
                in1=t_sb[:].to_broadcast([P, n, PACK]),
                op=ALU.mult,
            )

        def w_quant(k, g0, g1):
            cols = slice(g0 * P, g1 * P)
            quant(w_codes[k][:, cols], w_scales[k][:, cols], w_bf[k][:, cols, :].rearrange("p n r -> p (n r)"))

        def values(k, g):
            i, c = divmod(k, 2)
            cols = slice(g * P, (g + 1) * P)
            nc.tensor.matmul_mx(
                out=y_ps[i][:, 2 * g + c, :],
                lhsT=w_codes[k][:, cols].bitcast(FP8X4),
                lhsT_scale=w_scales[k][:, cols],
                rhs=v_codes[:, cols].bitcast(FP8X4),
                rhs_scale=v_scales[:, cols],
                start=True,
                stop=True,
            )

        def sigmoid(i):
            nc.scalar.activation(
                out=sig[i][:].rearrange("p x e -> p (x e)"), in_=og_sb[i][:].rearrange("p g x -> p (g x)"), func=ACT.Sigmoid
            )

        def gain(i):
            nc.vector.tensor_tensor(out=gate[i][:], in0=sig[i][:], in1=gn_sb[:].to_broadcast([P, 4, E]), op=ALU.mult)

        def square(i, x):
            nc.scalar.activation(
                out=squares[:, 4 * i + x], in_=y_ps[i][:, x, :], func=ACT.Square, accum_out=ssq[:, 4 * i + x : 4 * i + x + 1]
            )

        def root(a, b):
            nc.scalar.activation(out=rms[:, a:b], in_=ssq[:, a:b], func=ACT.Sqrt, scale=1.0 / E, bias=256.0 * 1e-5)

        def invert(a, b):
            nc.vector.reciprocal(out=rinv[:, a:b], in_=rms[:, a:b])

        def finish(i, x):
            g, c = divmod(x, 2)
            nc.vector.scalar_tensor_tensor(
                out=res[i][:, g, c * E : (c + 1) * E],
                in0=y_ps[i][:, x, :],
                scalar=rinv[:, 4 * i + x : 4 * i + x + 1],
                in1=gate[i][:, x],
                op0=ALU.mult,
                op1=ALU.mult,
            )

        def premul(i, x0, x1):
            nc.vector.tensor_tensor(out=gated[i][:, x0:x1], in0=y_ps[i][:, x0:x1, :], in1=gate[i][:, x0:x1], op=ALU.mult)

        def scale(i, x):
            g, c = divmod(x, 2)
            nc.scalar.activation(
                out=res[i][:, g, c * E : (c + 1) * E], in_=gated[i][:, x], func=ACT.Copy, scale=rinv[:, 4 * i + x : 4 * i + x + 1]
            )

        def rsqrt(a, b):
            nc.scalar.activation(out=rinv[:, a:b], in_=ssq[:, a:b], func=ACT.Abs_reciprocal_sqrt, scale=1.0 / E, bias=256.0 * 1e-5)

        def mean(a, b):
            nc.vector.tensor_scalar(
                out=rms[:, a:b], in0=ssq[:, a:b], scalar1=1.0 / E, scalar2=256.0 * 1e-5, op0=ALU.mult, op1=ALU.add
            )

        def power(a, b):
            nc.gpsimd.tensor_tensor(out=rinv[:, a:b], in0=rms[:, a:b], in1=expo[:, a:b], op=ALU.pow)

        def set_expo():
            nc.gpsimd.memset(expo[:], -0.5)

        def pgain(i, x0, x1):
            nc.gpsimd.tensor_tensor(
                out=gate[i][:, x0:x1], in0=sig[i][:, x0:x1], in1=gn_sb[:].to_broadcast([P, x1 - x0, E]), op=ALU.mult
            )

        def pscale(i, x):
            g, c = divmod(x, 2)
            nc.gpsimd.tensor_scalar(
                out=res[i][:, g, c * E : (c + 1) * E], in0=gated[i][:, x], scalar1=rinv[:, 4 * i + x : 4 * i + x + 1],
                scalar2=0.0, op0=ALU.mult, op1=ALU.add,
            )

        def store(i, g0, g1):
            if i == 0:
                nc.sync.dma_start(out=plain_rows(out, g0), in_=res[0][:, g0].rearrange("p (c e) -> p c e", c=2))
            else:
                nc.sync.dma_start(out=rows_of(out, i)[:, g0:g1], in_=res[i][:, g0:g1])

        do = dict(
            load_q=load_q, load_og=load_og, load_k=load_k, load_t=load_t, load_gn=load_gn, load_v=load_v, warm=warm,
            k_deal=k_deal, k_quant=k_quant, q_deal=q_deal, q_quant=q_quant, v_deal=v_deal, v_quant=v_quant,
            scores=scores, tanh=tanh, weigh=weigh, w_quant=w_quant, values=values, sigmoid=sigmoid, gain=gain,
            square=square, root=root, invert=invert, finish=finish, store=store, mean=mean, power=power, set_expo=set_expo, pgain=pgain, pscale=pscale, load_q_first=load_q_first, q_first_deal=q_first_deal, premul=premul, scale=scale, rsqrt=rsqrt,
        )
        for step in STEPS:
            do[step[0]](*step[1:])
